import numpy as np
import ml_dtypes


def mxq(x, axis, fmt="e4m3"):
    dtype, down = {"e4m3": (ml_dtypes.float8_e4m3fn, 7), "e5m2": (ml_dtypes.float8_e5m2, 14)}[fmt]
    v = np.moveaxis(np.asarray(x, np.float32).astype(ml_dtypes.bfloat16).astype(np.float64), axis, -1)
    blocks = v.reshape(v.shape[:-1] + (-1, 32))
    amax = np.abs(blocks).max(-1, keepdims=True)
    byte = np.maximum(np.where(amax > 0, np.frexp(amax)[1] - 1 + 127, 0) - down, 1)
    scale = np.exp2(byte - 127.0)
    codes = (blocks / scale).astype(np.float32).astype(dtype).astype(np.float64)
    return np.moveaxis((codes * scale).reshape(v.shape), -1, axis)


WIDE = False


def mx_kscale(k):
    if not WIDE:
        return np.ones(k)
    levels = np.array([10, -10, 5, -5, 0])
    if k % 512:
        return np.exp2(np.random.permutation(np.resize(levels, k // 32))).repeat(32)
    a = np.empty((k // 512, 16))
    for p in range(k // 512):
        a[p, :8] = np.random.permutation(np.resize(levels, 8))
        for g in range(8):
            far = levels[np.abs(levels - a[p, g]) >= 10]
            a[p, g + 8] = far[np.random.randint(len(far))]
    return np.exp2(a.ravel()).repeat(32)


def f64(x):
    return np.asarray(x).astype(np.float64)


def striped(idx):
    return np.tile(np.asarray(idx).reshape(-1, 16).T, (8, 1)).astype(np.uint16)


def unstriped(offs):
    return offs[:16].T.reshape(-1).astype(np.int64)


E2M1 = np.array([0.0, 0.5, 1.0, 1.5, 2.0, 3.0, 4.0, 6.0, -0.0, -0.5, -1.0, -1.5, -2.0, -3.0, -4.0, -6.0])


def pack_weight(w, fmt):
    k, n = w.shape
    w = f64(np.asarray(w, np.float32).astype(ml_dtypes.bfloat16)).reshape(k // 32, 32, n)
    amax = np.abs(w).max(1)
    if fmt == "e4m3":
        byte = np.frexp(amax)[1] - 1 + 127 - 7
    else:
        mant, ex = np.frexp(amax / 6.0)
        byte = np.where(mant > 0.5, ex, ex - 1) + 127
    byte = np.clip(np.where(amax > 0, byte, 1), 1, 254)
    scaled = (w * np.exp2(127.0 - byte)[:, None, :]).reshape(k, n).astype(np.float32)
    by_word = np.ascontiguousarray(scaled.reshape(k // 512, 128, 4, n).transpose(0, 1, 3, 2))
    if fmt == "e4m3":
        words = by_word.astype(ml_dtypes.float8_e4m3fn).view(np.uint8)
    else:
        c = by_word.astype(ml_dtypes.float4_e2m1fn).view(np.uint8) & 0xF
        words = (c[..., 0::2] | (c[..., 1::2] << 4)).reshape(k // 512, 128, 2 * n)
    return np.ascontiguousarray(words), np.ascontiguousarray(byte.astype(np.uint8).reshape(k // 512, 16, n))


def unpack_weight(words, scales, fmt):
    g, _, n = scales.shape
    words = np.ascontiguousarray(words).reshape(g, 128, n, -1)
    if fmt == "e4m3":
        vals = words.view(ml_dtypes.float8_e4m3fn).astype(np.float64)
    else:
        nib = np.empty((g, 128, n, 4), np.uint8)
        nib[..., 0::2] = words & 0xF
        nib[..., 1::2] = words >> 4
        vals = E2M1[nib]
    vals = vals * np.repeat(np.exp2(scales.astype(np.float64) - 127.0), 8, axis=1)[..., None]
    return vals.transpose(0, 1, 3, 2).reshape(g * 512, n)


def bf(x):
    return np.asarray(x, np.float32).astype(ml_dtypes.bfloat16)


def planes(Y):
    r, m = Y.shape
    b = f64(bf(Y)).reshape(r // 32, 32, m)
    amax = np.abs(b).max(1)
    byte = np.clip(np.where(amax > 0, np.frexp(amax)[1] - 1 + 127 - 7, 1), 1, 254)
    codes = (b * np.exp2(127.0 - byte)[:, None, :]).reshape(r, m).astype(np.float32).astype(ml_dtypes.float8_e4m3fn).view(np.uint8)
    words = codes.reshape(r // 512, 128, 4, m).transpose(0, 1, 3, 2)
    return np.ascontiguousarray(words), np.ascontiguousarray(byte.astype(np.uint8).reshape(r // 512, 16, m))


K, T, I, C, J, N = 512, 1024, 512, 1024, 512, 512


def setup_inputs():
    n = np.random.standard_normal
    idx = np.random.permutation(C)[:J]
    idx2 = np.random.permutation(T)[:I]
    fk = mx_kscale(K)
    fj = mx_kscale(J)
    xtp = pack_weight(n((K, T)) * np.random.uniform(0.2, 2.0, (1, T)) / fk[:, None], "e4m3")
    wcp = pack_weight(n((K, C)) * 1 / np.sqrt(K) * fk[:, None], "e2m1")
    wop = pack_weight(n((J, N)) * 1 / np.sqrt(J) / fj[:, None], "e4m3")
    return {
        "xt_words": xtp[0],
        "xt_scales": xtp[1],
        "wc_words": wcp[0],
        "wc_scales": wcp[1],
        "fj": (np.random.uniform(0.5, 2.0, (J, 1)) * fj[:, None]).astype(np.float32),
        "wo_words": wop[0],
        "wo_scales": wop[1],
        "offs": striped(idx),
        "offs2": striped(idx2),
    }


def reference(xt_words, xt_scales, wc_words, wc_scales, fj, wo_words, wo_scales, offs, offs2):
    idx = unstriped(offs)
    idx2 = unstriped(offs2)
    xtu = unpack_weight(xt_words, xt_scales, "e4m3")
    wcu = unpack_weight(wc_words, wc_scales, "e2m1")
    wou = unpack_weight(wo_words, wo_scales, "e4m3")
    xtidx2g = xtu[:, idx2]
    z = xtidx2g.T @ wcu
    u = z * 1.0 / np.sqrt(np.mean(np.square(z), axis=1, keepdims=True) + 0.01)
    us1 = u[:, idx]
    ut = us1.T
    uw = ut * f64(fj)
    uwq = mxq(uw, 0, "e4m3")
    y = wou.T @ uwq
    words, scales = planes(y)
    return y, words, scales

@@ -1,0 +1,214 @@
+from contextlib import ExitStack
+
+import concourse.mybir as mybir
+from concourse.masks import make_identity
+
+K, T, I, C, J, N = 512, 1024, 512, 1024, 512, 512
+FLOPS = 2 * K * I * C + 2 * J * N * I
+
+F32 = mybir.dt.float32
+BF16 = mybir.dt.bfloat16
+I32 = mybir.dt.int32
+U32 = mybir.dt.uint32
+U16 = mybir.dt.uint16
+U8 = mybir.dt.uint8
+FP8X4 = mybir.dt.float8_e4m3fn_x4
+FP4X4 = mybir.dt.float4_e2m1fn_x4
+ACT = mybir.ActivationFunctionType
+ALU = mybir.AluOpType
+
+P = 128
+PACK = 4
+BANK = 512
+TILES = I // P
+EPS = 0.01
+ON_VECTOR = ((3, 1),)
+
+
+def load_scale_rows(queue, plane, rows, quadrant):
+    queue.dma_start(
+        out=plane[32 * quadrant : 32 * quadrant + 4, :].bitcast(I32),
+        in_=rows[4 * quadrant : 4 * quadrant + 4, :].bitcast(I32),
+    )
+
+
+def tile_list_unit_rows_listed_features_pl_kernel(
+    tc, xt_words, xt_scales, wc_words, wc_scales, fj, wo_words, wo_scales, offs, offs2, out_0, out_1, out_2
+):
+    nc = tc.nc
+    with ExitStack() as ctx:
+        keep = ctx.enter_context(tc.tile_pool(name="keep", bufs=1))
+        work = ctx.enter_context(tc.tile_pool(name="work", bufs=4))
+        psum = ctx.enter_context(tc.psum_pool(name="psum", bufs=8))
+
+        token_list = keep.tile([P, I // 16], U16)
+        feature_list = keep.tile([P, J // 16], U16)
+        x_words = keep.tile([P, T], I32, align_bytes=64)
+        x_plane = keep.tile([P, T], U8, align_bytes=64)
+        wc_codes = keep.tile([P, 2 * C], U8, align_bytes=64)
+        wc_plane = keep.tile([P, C], U8, align_bytes=64)
+        wo_raw = keep.tile([P, N], I32, align_bytes=64)
+        wo_raw_plane = keep.tile([P, N], U8, align_bytes=64)
+        wo_codes = keep.tile([P, N], I32, align_bytes=64)
+        wo_plane = keep.tile([P, N], U8, align_bytes=64)
+        fj_cols = keep.tile([P, PACK], F32)
+        fj_row = keep.tile([P, J], F32)
+        z_first = keep.tile([P, C], F32)
+        ident = keep.tile([P, P], F32)
+        warm_in = keep.tile([P, 1], F32)
+        warm_out = keep.tile([P, 1], F32)
+        y_words = keep.tile([P, I], I32, align_bytes=64)
+        y_plane = keep.tile([P, I], U8, align_bytes=64)
+
+        nc.vector.memset(x_plane[:].bitcast(I32), 0)
+        nc.vector.memset(wc_plane[:].bitcast(I32), 0)
+        nc.vector.memset(warm_in[:], 1.0)
+        nc.vector.memset(wo_raw_plane[:].bitcast(I32), 0)
+
+        nc.sync.dma_start(token_list[:], offs2)
+        for q in range(4):
+            load_scale_rows(nc.scalar if q < 2 else nc.sync, x_plane, xt_scales[0], q)
+        nc.scalar.dma_start(out=fj_cols[:], in_=fj.rearrange("(p t) o -> p (t o)", t=PACK))
+        nc.sync.dma_start(out=x_words[:], in_=xt_words[0].rearrange("p n t -> p (n t)").bitcast(I32))
+        nc.sync.dma_start(out=wc_codes[:].bitcast(I32), in_=wc_words[0].bitcast(I32))
+        for q in range(4):
+            load_scale_rows(nc.sync, wc_plane, wc_scales[0], q)
+        nc.sync.dma_start(feature_list[:], offs)
+        nc.sync.dma_start(out=wo_raw[:], in_=wo_words[0].rearrange("p n t -> p (n t)").bitcast(I32))
+        for q in range(4):
+            load_scale_rows(nc.sync, wo_raw_plane, wo_scales[0], q)
+
+        nc.scalar.activation(out=warm_out[:], in_=warm_in[:], func=ACT.Abs_reciprocal_sqrt)
+        make_identity(nc, ident[:])
+
+        xg_words, xg_plane = [], []
+        for ti in range(TILES):
+            picks = token_list[:, 8 * ti : 8 * ti + 8]
+            xg_plane.append(work.tile([P, P], U8, align_bytes=64, name="xg_plane"))
+            nc.vector.tensor_copy(out=xg_plane[ti][:], in_=x_plane[:].indirect(picks))
+            xg_words.append(work.tile([P, P], I32, align_bytes=64, name="xg_words"))
+            nc.vector.tensor_copy(out=xg_words[ti][:].bitcast(U32), in_=x_words[:].bitcast(U32).indirect(picks))
+
+        spread = psum.tile([P, PACK, P], F32, name="bank")
+        for t in range(PACK):
+            nc.tensor.transpose(spread[:, t, :], fj_cols[:, t : t + 1].to_broadcast([P, P]), ident[:])
+        nc.scalar.copy(out=fj_row[:].rearrange("p (m t) -> p m t", t=PACK), in_=spread[:].rearrange("p t m -> p m t"))
+
+        y_tiles = {}
+        z_banks, u_tiles, inv_rms, picked, uw_words, uw_plane = {}, {}, {}, {}, {}, {}
+
+        def first_product(ti):
+            z_banks[ti] = []
+            for h in range(C // BANK):
+                bank = psum.tile([P, BANK], F32, name="bank")
+                nc.tensor.matmul_mx(
+                    out=bank[:],
+                    lhsT=xg_words[ti][:].bitcast(FP8X4),
+                    lhsT_scale=xg_plane[ti][:],
+                    rhs=wc_codes[:, 2 * BANK * h : 2 * BANK * (h + 1)].bitcast(FP4X4),
+                    rhs_scale=wc_plane[:, BANK * h : BANK * (h + 1)],
+                    start=True,
+                    stop=True,
+                )
+                z_banks[ti].append(bank)
+
+        def row_statistics(ti):
+            stats = work.tile([P, 4], F32, name="stats")
+            for h in range(C // BANK):
+                squares = work.tile([P, BANK], BF16, name="squares")
+                nc.scalar.activation(
+                    out=squares[:], in_=z_banks[ti][h][:], func=ACT.Square, scale=C**-0.5, accum_out=stats[:, h : h + 1]
+                )
+                if h == 0:
+                    nc.scalar.activation(out=stats[:, 2:3], in_=stats[:, 0:1], func=ACT.Copy, bias=EPS)
+                if ti == 0:
+                    nc.vector.tensor_copy(out=z_first[:, BANK * h : BANK * (h + 1)], in_=z_banks[ti][h][:])
+            nc.scalar.activation(out=stats[:, 3:4], in_=stats[:, 1:2], func=ACT.Abs_reciprocal_sqrt, bias=stats[:, 2:3])
+            inv_rms[ti] = stats[:, 3:4]
+
+        def normalise(ti):
+            u_tiles[ti] = work.tile([P, C], F32, name="u")
+            if ti == 0:
+                nc.vector.tensor_scalar(out=u_tiles[ti][:], in0=z_first[:], scalar1=inv_rms[ti], scalar2=None, op0=ALU.mult)
+                return
+            for h in range(C // BANK):
+                half = u_tiles[ti][:, BANK * h : BANK * (h + 1)]
+                if (ti, h) in ON_VECTOR:
+                    nc.vector.tensor_scalar(out=half, in0=z_banks[ti][h][:], scalar1=inv_rms[ti], scalar2=None, op0=ALU.mult)
+                else:
+                    nc.scalar.activation(out=half, in_=z_banks[ti][h][:], func=ACT.Copy, scale=inv_rms[ti])
+
+        def pick(ti):
+            picked[ti] = work.tile([P, J], F32, name="picked")
+            nc.vector.tensor_tensor(out=picked[ti][:], in0=u_tiles[ti][:].indirect(feature_list[:]), in1=fj_row[:], op=ALU.mult)
+
+        def turn(ti):
+            rounded = work.tile([P, J], BF16, name="rounded")
+            nc.vector.tensor_copy(out=rounded[:], in_=picked[ti][:])
+            pairs = rounded[:].bitcast(F32)
+            turned = psum.tile([P, 2, P], F32, name="bank")
+            for e in range(2):
+                nc.tensor.transpose(turned[:, e, :], pairs[:, e : J // 2 : 2], ident[:])
+            grouped = work.tile([P, P * PACK], BF16, align_bytes=64, name="grouped")
+            nc.scalar.copy(
+                out=grouped[:].bitcast(F32).rearrange("p (i e) -> p i e", e=2), in_=turned[:].rearrange("p e i -> p i e")
+            )
+            uw_words[ti] = work.tile([P, P], I32, align_bytes=64, name="uw_words")
+            uw_plane[ti] = work.tile([P, P], U8, align_bytes=64, name="uw_plane")
+            nc.vector.quantize_mx(out=uw_words[ti][:].bitcast(FP8X4), scales=uw_plane[ti][:], in_=grouped[:])
+
+        def second_product(ti):
+            cols = slice(P * ti, P * (ti + 1))
+            bank = psum.tile([P, PACK, P], F32, name="bank")
+            for t in range(PACK):
+                nc.tensor.matmul_mx(
+                    out=bank[:, t, :],
+                    lhsT=wo_codes[:, P * t : P * (t + 1)].bitcast(FP8X4),
+                    lhsT_scale=wo_plane[:, P * t : P * (t + 1)],
+                    rhs=uw_words[ti][:].bitcast(FP8X4),
+                    rhs_scale=uw_plane[ti][:],
+                    start=True,
+                    stop=True,
+                )
+            y = work.tile([P, PACK, P], F32, name="y")
+            nc.scalar.copy(out=y[:], in_=bank[:])
+            nc.sync.dma_start(out=out_0.rearrange("(p t) i -> p t i", t=PACK)[:, :, cols], in_=y[:])
+            y_tiles[ti] = y
+
+        def planes(ti):
+            cols = slice(P * ti, P * (ti + 1))
+            y = y_tiles[ti]
+            y_grouped = work.tile([P, P * PACK], BF16, align_bytes=64, name="y_grouped")
+            nc.vector.tensor_copy(
+                out=y_grouped[:].rearrange("p (c i t) -> p c t i", i=4, t=PACK),
+                in_=y[:].rearrange("p t (c i) -> p c t i", i=4),
+            )
+            nc.vector.quantize_mx(out=y_words[:, cols].bitcast(FP8X4), scales=y_plane[:, cols], in_=y_grouped[:])
+            nc.sync.dma_start(out=out_1[0].rearrange("p i t -> p (i t)").bitcast(I32)[:, cols], in_=y_words[:, cols])
+
+        for ti in range(TILES):
+            first_product(ti)
+        nc.vector.tensor_copy(
+            out=wo_codes[:].rearrange("p (t m) -> p t m", t=PACK), in_=wo_raw[:].rearrange("p (m t) -> p t m", t=PACK)
+        )
+        nc.vector.tensor_copy(
+            out=wo_plane[:].rearrange("p (t m) -> p t m", t=PACK), in_=wo_raw_plane[:].rearrange("p (m t) -> p t m", t=PACK)
+        )
+        for ti in range(TILES):
+            row_statistics(ti)
+            if ti == TILES - 1:
+                turn(0)
+                turn(1)
+            normalise(ti)
+            pick(ti)
+        turn(2)
+        turn(3)
+        for ti in range(TILES):
+            second_product(ti)
+        for ti in range(TILES):
+            planes(ti)
+
+        for q in range(4):
+            (nc.sync if q % 2 else nc.scalar).dma_start(
+                out=out_2[0][4 * q : 4 * q + 4, :].bitcast(I32), in_=y_plane[32 * q : 32 * q + 4, :].bitcast(I32)
+            )

@@ -22,7 +22,7 @@ PACK = 4
 BANK = 512
 TILES = I // P
 EPS = 0.01
-ON_VECTOR = ((3, 1),)
+ON_VECTOR = ((0, 0), (0, 1), (2, 1))
 
 
 def load_scale_rows(queue, plane, rows, quadrant):
@@ -39,6 +39,8 @@ def tile_list_unit_rows_listed_features_pl_kernel(
     with ExitStack() as ctx:
         keep = ctx.enter_context(tc.tile_pool(name="keep", bufs=1))
         work = ctx.enter_context(tc.tile_pool(name="work", bufs=4))
+        vector_ring = ctx.enter_context(tc.tile_pool(name="vector_ring", bufs=28))
+        scalar_ring = ctx.enter_context(tc.tile_pool(name="scalar_ring", bufs=8))
         psum = ctx.enter_context(tc.psum_pool(name="psum", bufs=8))
 
         token_list = keep.tile([P, I // 16], U16)
@@ -49,11 +51,8 @@ def tile_list_unit_rows_listed_features_pl_kernel(
         wc_plane = keep.tile([P, C], U8, align_bytes=64)
         wo_raw = keep.tile([P, N], I32, align_bytes=64)
         wo_raw_plane = keep.tile([P, N], U8, align_bytes=64)
-        wo_codes = keep.tile([P, N], I32, align_bytes=64)
-        wo_plane = keep.tile([P, N], U8, align_bytes=64)
         fj_cols = keep.tile([P, PACK], F32)
         fj_row = keep.tile([P, J], F32)
-        z_first = keep.tile([P, C], F32)
         ident = keep.tile([P, P], F32)
         warm_in = keep.tile([P, 1], F32)
         warm_out = keep.tile([P, 1], F32)
@@ -81,12 +80,18 @@ def tile_list_unit_rows_listed_features_pl_kernel(
         nc.scalar.activation(out=warm_out[:], in_=warm_in[:], func=ACT.Abs_reciprocal_sqrt)
         make_identity(nc, ident[:])
 
-        xg_words, xg_plane = [], []
+        def vector_tile(shape, dtype, name):
+            return vector_ring.tile(shape, dtype, align_bytes=64, name=name, tag="vector")
+
+        def scalar_tile(shape, dtype, name):
+            return scalar_ring.tile(shape, dtype, align_bytes=64, name=name, tag="scalar")
+
+        xg_plane = vector_tile([P, I], U8, "xg_plane")
+        nc.vector.tensor_copy(out=xg_plane[:], in_=x_plane[:].indirect(token_list[:]))
+        xg_words = []
         for ti in range(TILES):
             picks = token_list[:, 8 * ti : 8 * ti + 8]
-            xg_plane.append(work.tile([P, P], U8, align_bytes=64, name="xg_plane"))
-            nc.vector.tensor_copy(out=xg_plane[ti][:], in_=x_plane[:].indirect(picks))
-            xg_words.append(work.tile([P, P], I32, align_bytes=64, name="xg_words"))
+            xg_words.append(vector_tile([P, P], I32, "xg_words"))
             nc.vector.tensor_copy(out=xg_words[ti][:].bitcast(U32), in_=x_words[:].bitcast(U32).indirect(picks))
 
         spread = psum.tile([P, PACK, P], F32, name="bank")
@@ -94,7 +99,7 @@ def tile_list_unit_rows_listed_features_pl_kernel(
             nc.tensor.transpose(spread[:, t, :], fj_cols[:, t : t + 1].to_broadcast([P, P]), ident[:])
         nc.scalar.copy(out=fj_row[:].rearrange("p (m t) -> p m t", t=PACK), in_=spread[:].rearrange("p t m -> p m t"))
 
-        y_tiles = {}
+        y_tiles, rounded, z_first = {}, {}, []
         z_banks, u_tiles, inv_rms, picked, uw_words, uw_plane = {}, {}, {}, {}, {}, {}
 
         def first_product(ti):
@@ -104,7 +109,7 @@ def tile_list_unit_rows_listed_features_pl_kernel(
                 nc.tensor.matmul_mx(
                     out=bank[:],
                     lhsT=xg_words[ti][:].bitcast(FP8X4),
-                    lhsT_scale=xg_plane[ti][:],
+                    lhsT_scale=xg_plane[:, P * ti : P * (ti + 1)],
                     rhs=wc_codes[:, 2 * BANK * h : 2 * BANK * (h + 1)].bitcast(FP4X4),
                     rhs_scale=wc_plane[:, BANK * h : BANK * (h + 1)],
                     start=True,
@@ -122,38 +127,38 @@ def tile_list_unit_rows_listed_features_pl_kernel(
                 if h == 0:
                     nc.scalar.activation(out=stats[:, 2:3], in_=stats[:, 0:1], func=ACT.Copy, bias=EPS)
                 if ti == 0:
-                    nc.vector.tensor_copy(out=z_first[:, BANK * h : BANK * (h + 1)], in_=z_banks[ti][h][:])
+                    z_first.append(vector_tile([P, BANK], F32, "z_first"))
+                    nc.vector.tensor_copy(out=z_first[h][:], in_=z_banks[ti][h][:])
             nc.scalar.activation(out=stats[:, 3:4], in_=stats[:, 1:2], func=ACT.Abs_reciprocal_sqrt, bias=stats[:, 2:3])
             inv_rms[ti] = stats[:, 3:4]
 
         def normalise(ti):
-            u_tiles[ti] = work.tile([P, C], F32, name="u")
-            if ti == 0:
-                nc.vector.tensor_scalar(out=u_tiles[ti][:], in0=z_first[:], scalar1=inv_rms[ti], scalar2=None, op0=ALU.mult)
-                return
+            u_tiles[ti] = vector_tile([P, C], F32, "u") if (ti, 1) in ON_VECTOR else work.tile([P, C], F32, name="u")
             for h in range(C // BANK):
                 half = u_tiles[ti][:, BANK * h : BANK * (h + 1)]
                 if (ti, h) in ON_VECTOR:
-                    nc.vector.tensor_scalar(out=half, in0=z_banks[ti][h][:], scalar1=inv_rms[ti], scalar2=None, op0=ALU.mult)
+                    nc.vector.tensor_scalar(out=half, in0=z_first[h][:] if ti == 0 else z_banks[ti][h][:], scalar1=inv_rms[ti], scalar2=None, op0=ALU.mult)
                 else:
                     nc.scalar.activation(out=half, in_=z_banks[ti][h][:], func=ACT.Copy, scale=inv_rms[ti])
 
         def pick(ti):
-            picked[ti] = work.tile([P, J], F32, name="picked")
+            picked[ti] = vector_tile([P, J], F32, "picked")
             nc.vector.tensor_tensor(out=picked[ti][:], in0=u_tiles[ti][:].indirect(feature_list[:]), in1=fj_row[:], op=ALU.mult)
 
+        def round_once(ti):
+            rounded[ti] = vector_tile([P, J], BF16, "rounded")
+            nc.vector.tensor_copy(out=rounded[ti][:], in_=picked[ti][:])
+
         def turn(ti):
-            rounded = work.tile([P, J], BF16, name="rounded")
-            nc.vector.tensor_copy(out=rounded[:], in_=picked[ti][:])
-            pairs = rounded[:].bitcast(F32)
+            pairs = rounded[ti][:].bitcast(F32)
             turned = psum.tile([P, 2, P], F32, name="bank")
             for e in range(2):
                 nc.tensor.transpose(turned[:, e, :], pairs[:, e : J // 2 : 2], ident[:])
-            grouped = work.tile([P, P * PACK], BF16, align_bytes=64, name="grouped")
+            grouped = scalar_tile([P, P * PACK], BF16, "grouped")
             nc.scalar.copy(
                 out=grouped[:].bitcast(F32).rearrange("p (i e) -> p i e", e=2), in_=turned[:].rearrange("p e i -> p i e")
             )
-            uw_words[ti] = work.tile([P, P], I32, align_bytes=64, name="uw_words")
+            uw_words[ti] = vector_tile([P, P], I32, "uw_words")
             uw_plane[ti] = work.tile([P, P], U8, align_bytes=64, name="uw_plane")
             nc.vector.quantize_mx(out=uw_words[ti][:].bitcast(FP8X4), scales=uw_plane[ti][:], in_=grouped[:])
 
@@ -170,7 +175,7 @@ def tile_list_unit_rows_listed_features_pl_kernel(
                     start=True,
                     stop=True,
                 )
-            y = work.tile([P, PACK, P], F32, name="y")
+            y = scalar_tile([P, PACK, P], F32, "y")
             nc.scalar.copy(out=y[:], in_=bank[:])
             nc.sync.dma_start(out=out_0.rearrange("(p t) i -> p t i", t=PACK)[:, :, cols], in_=y[:])
             y_tiles[ti] = y
@@ -178,7 +183,7 @@ def tile_list_unit_rows_listed_features_pl_kernel(
         def planes(ti):
             cols = slice(P * ti, P * (ti + 1))
             y = y_tiles[ti]
-            y_grouped = work.tile([P, P * PACK], BF16, align_bytes=64, name="y_grouped")
+            y_grouped = vector_tile([P, P * PACK], BF16, "y_grouped")
             nc.vector.tensor_copy(
                 out=y_grouped[:].rearrange("p (c i t) -> p c t i", i=4, t=PACK),
                 in_=y[:].rearrange("p t (c i) -> p c t i", i=4),
@@ -188,25 +193,30 @@ def tile_list_unit_rows_listed_features_pl_kernel(
 
         for ti in range(TILES):
             first_product(ti)
+        wo_codes = vector_tile([P, N], I32, "wo_codes")
         nc.vector.tensor_copy(
-            out=wo_codes[:].rearrange("p (t m) -> p t m", t=PACK), in_=wo_raw[:].rearrange("p (m t) -> p t m", t=PACK)
+            out=wo_codes[:].rearrange("p (t c i) -> p c t i", t=PACK, i=4),
+            in_=wo_raw[:].rearrange("p (c i t) -> p c t i", t=PACK, i=4),
         )
+        row_statistics(0)
+        wo_plane = vector_tile([P, N], U8, "wo_plane")
         nc.vector.tensor_copy(
             out=wo_plane[:].rearrange("p (t m) -> p t m", t=PACK), in_=wo_raw_plane[:].rearrange("p (m t) -> p t m", t=PACK)
         )
-        for ti in range(TILES):
-            row_statistics(ti)
-            if ti == TILES - 1:
-                turn(0)
-                turn(1)
-            normalise(ti)
-            pick(ti)
-        turn(2)
-        turn(3)
-        for ti in range(TILES):
-            second_product(ti)
-        for ti in range(TILES):
-            planes(ti)
+        normalise(0)
+        row_statistics(1)
+        for step in range(TILES + 4):
+            for stage, ti in (
+                (pick, step),
+                (turn, step - 2),
+                (normalise, step + 1),
+                (row_statistics, step + 2),
+                (round_once, step),
+                (planes, step - 4),
+                (second_product, step - 3),
+            ):
+                if 0 <= ti < TILES:
+                    stage(ti)
 
         for q in range(4):
             (nc.sync if q % 2 else nc.scalar).dma_start(

@@ -22,7 +22,7 @@ PACK = 4
 BANK = 512
 TILES = I // P
 EPS = 0.01
-ON_VECTOR = ((0, 0), (0, 1), (2, 1))
+ON_VECTOR = ((0, 0), (0, 1), (1, 1), (2, 1))
 
 
 def load_scale_rows(queue, plane, rows, quadrant):
@@ -40,7 +40,7 @@ def tile_list_unit_rows_listed_features_pl_kernel(
         keep = ctx.enter_context(tc.tile_pool(name="keep", bufs=1))
         work = ctx.enter_context(tc.tile_pool(name="work", bufs=4))
         vector_ring = ctx.enter_context(tc.tile_pool(name="vector_ring", bufs=28))
-        scalar_ring = ctx.enter_context(tc.tile_pool(name="scalar_ring", bufs=8))
+        scalar_ring = ctx.enter_context(tc.tile_pool(name="scalar_ring", bufs=9))
         psum = ctx.enter_context(tc.psum_pool(name="psum", bufs=8))
 
         token_list = keep.tile([P, I // 16], U16)
@@ -99,7 +99,7 @@ def tile_list_unit_rows_listed_features_pl_kernel(
             nc.tensor.transpose(spread[:, t, :], fj_cols[:, t : t + 1].to_broadcast([P, P]), ident[:])
         nc.scalar.copy(out=fj_row[:].rearrange("p (m t) -> p m t", t=PACK), in_=spread[:].rearrange("p t m -> p m t"))
 
-        y_tiles, rounded, z_first = {}, {}, []
+        y_tiles, rounded, grouped, z_first = {}, {}, {}, []
         z_banks, u_tiles, inv_rms, picked, uw_words, uw_plane = {}, {}, {}, {}, {}, {}
 
         def first_product(ti):
@@ -133,7 +133,7 @@ def tile_list_unit_rows_listed_features_pl_kernel(
             inv_rms[ti] = stats[:, 3:4]
 
         def normalise(ti):
-            u_tiles[ti] = vector_tile([P, C], F32, "u") if (ti, 1) in ON_VECTOR else work.tile([P, C], F32, name="u")
+            u_tiles[ti] = vector_tile([P, C], F32, "u") if (ti, 1) in ON_VECTOR else scalar_tile([P, C], F32, "u")
             for h in range(C // BANK):
                 half = u_tiles[ti][:, BANK * h : BANK * (h + 1)]
                 if (ti, h) in ON_VECTOR:
@@ -147,20 +147,25 @@ def tile_list_unit_rows_listed_features_pl_kernel(
 
         def round_once(ti):
             rounded[ti] = vector_tile([P, J], BF16, "rounded")
-            nc.vector.tensor_copy(out=rounded[ti][:], in_=picked[ti][:])
+            nc.vector.tensor_copy(
+                out=rounded[ti][:].rearrange("p (e m k) -> p e m k", e=2, k=2),
+                in_=picked[ti][:].rearrange("p (m e k) -> p e m k", e=2, k=2),
+            )
 
         def turn(ti):
             pairs = rounded[ti][:].bitcast(F32)
             turned = psum.tile([P, 2, P], F32, name="bank")
             for e in range(2):
-                nc.tensor.transpose(turned[:, e, :], pairs[:, e : J // 2 : 2], ident[:])
-            grouped = scalar_tile([P, P * PACK], BF16, "grouped")
+                nc.tensor.transpose(turned[:, e, :], pairs[:, P * e : P * (e + 1)], ident[:])
+            grouped[ti] = scalar_tile([P, P * PACK], BF16, "grouped")
             nc.scalar.copy(
-                out=grouped[:].bitcast(F32).rearrange("p (i e) -> p i e", e=2), in_=turned[:].rearrange("p e i -> p i e")
+                out=grouped[ti][:].bitcast(F32).rearrange("p (i e) -> p i e", e=2), in_=turned[:].rearrange("p e i -> p i e")
             )
+
+        def quantise(ti):
             uw_words[ti] = vector_tile([P, P], I32, "uw_words")
             uw_plane[ti] = work.tile([P, P], U8, align_bytes=64, name="uw_plane")
-            nc.vector.quantize_mx(out=uw_words[ti][:].bitcast(FP8X4), scales=uw_plane[ti][:], in_=grouped[:])
+            nc.vector.quantize_mx(out=uw_words[ti][:].bitcast(FP8X4), scales=uw_plane[ti][:], in_=grouped[ti][:])
 
         def second_product(ti):
             cols = slice(P * ti, P * (ti + 1))
@@ -189,7 +194,9 @@ def tile_list_unit_rows_listed_features_pl_kernel(
                 in_=y[:].rearrange("p t (c i) -> p c t i", i=4),
             )
             nc.vector.quantize_mx(out=y_words[:, cols].bitcast(FP8X4), scales=y_plane[:, cols], in_=y_grouped[:])
-            nc.sync.dma_start(out=out_1[0].rearrange("p i t -> p (i t)").bitcast(I32)[:, cols], in_=y_words[:, cols])
+            if ti != 1:
+                span = slice(P * (ti - (ti == 2)), P * (ti + 1))
+                nc.sync.dma_start(out=out_1[0].rearrange("p i t -> p (i t)").bitcast(I32)[:, span], in_=y_words[:, span])
 
         for ti in range(TILES):
             first_product(ti)
@@ -208,12 +215,13 @@ def tile_list_unit_rows_listed_features_pl_kernel(
         for step in range(TILES + 4):
             for stage, ti in (
                 (pick, step),
-                (turn, step - 2),
-                (normalise, step + 1),
                 (row_statistics, step + 2),
-                (round_once, step),
+                (normalise, step + 1),
+                (turn, step - 1),
+                (quantise, step - 2),
                 (planes, step - 4),
                 (second_product, step - 3),
+                (round_once, step),
             ):
                 if 0 <= ti < TILES:
                     stage(ti)

@@ -52,7 +52,6 @@ def tile_list_unit_rows_listed_features_pl_kernel(
         wo_raw = keep.tile([P, N], I32, align_bytes=64)
         wo_raw_plane = keep.tile([P, N], U8, align_bytes=64)
         fj_cols = keep.tile([P, PACK], F32)
-        fj_row = keep.tile([P, J], F32)
         ident = keep.tile([P, P], F32)
         warm_in = keep.tile([P, 1], F32)
         warm_out = keep.tile([P, 1], F32)
@@ -67,7 +66,6 @@ def tile_list_unit_rows_listed_features_pl_kernel(
         nc.sync.dma_start(token_list[:], offs2)
         for q in range(4):
             load_scale_rows(nc.scalar if q < 2 else nc.sync, x_plane, xt_scales[0], q)
-        nc.scalar.dma_start(out=fj_cols[:], in_=fj.rearrange("(p t) o -> p (t o)", t=PACK))
         nc.sync.dma_start(out=x_words[:], in_=xt_words[0].rearrange("p n t -> p (n t)").bitcast(I32))
         nc.sync.dma_start(out=wc_codes[:].bitcast(I32), in_=wc_words[0].bitcast(I32))
         for q in range(4):
@@ -76,6 +74,7 @@ def tile_list_unit_rows_listed_features_pl_kernel(
         nc.sync.dma_start(out=wo_raw[:], in_=wo_words[0].rearrange("p n t -> p (n t)").bitcast(I32))
         for q in range(4):
             load_scale_rows(nc.sync, wo_raw_plane, wo_scales[0], q)
+        nc.sync.dma_start(out=fj_cols[:], in_=fj.rearrange("(p t) o -> p (t o)", t=PACK))
 
         nc.scalar.activation(out=warm_out[:], in_=warm_in[:], func=ACT.Abs_reciprocal_sqrt)
         make_identity(nc, ident[:])
@@ -94,12 +93,7 @@ def tile_list_unit_rows_listed_features_pl_kernel(
             xg_words.append(vector_tile([P, P], I32, "xg_words"))
             nc.vector.tensor_copy(out=xg_words[ti][:].bitcast(U32), in_=x_words[:].bitcast(U32).indirect(picks))
 
-        spread = psum.tile([P, PACK, P], F32, name="bank")
-        for t in range(PACK):
-            nc.tensor.transpose(spread[:, t, :], fj_cols[:, t : t + 1].to_broadcast([P, P]), ident[:])
-        nc.scalar.copy(out=fj_row[:].rearrange("p (m t) -> p m t", t=PACK), in_=spread[:].rearrange("p t m -> p m t"))
-
-        y_tiles, rounded, grouped, z_first = {}, {}, {}, []
+        y_tiles, turned, grouped, z_first = {}, {}, {}, []
         z_banks, u_tiles, inv_rms, picked, uw_words, uw_plane = {}, {}, {}, {}, {}, {}
 
         def first_product(ti):
@@ -143,23 +137,20 @@ def tile_list_unit_rows_listed_features_pl_kernel(
 
         def pick(ti):
             picked[ti] = vector_tile([P, J], F32, "picked")
-            nc.vector.tensor_tensor(out=picked[ti][:], in0=u_tiles[ti][:].indirect(feature_list[:]), in1=fj_row[:], op=ALU.mult)
-
-        def round_once(ti):
-            rounded[ti] = vector_tile([P, J], BF16, "rounded")
-            nc.vector.tensor_copy(
-                out=rounded[ti][:].rearrange("p (e m k) -> p e m k", e=2, k=2),
-                in_=picked[ti][:].rearrange("p (m e k) -> p e m k", e=2, k=2),
-            )
+            nc.vector.tensor_copy(out=picked[ti][:], in_=u_tiles[ti][:].indirect(feature_list[:]))
 
         def turn(ti):
-            pairs = rounded[ti][:].bitcast(F32)
-            turned = psum.tile([P, 2, P], F32, name="bank")
-            for e in range(2):
-                nc.tensor.transpose(turned[:, e, :], pairs[:, P * e : P * (e + 1)], ident[:])
-            grouped[ti] = scalar_tile([P, P * PACK], BF16, "grouped")
-            nc.scalar.copy(
-                out=grouped[ti][:].bitcast(F32).rearrange("p (i e) -> p i e", e=2), in_=turned[:].rearrange("p e i -> p i e")
+            turned[ti] = psum.tile([P, PACK, P], F32, name="bank")
+            for t in range(PACK):
+                nc.tensor.transpose(turned[ti][:, t, :], picked[ti][:, t:J:PACK], ident[:])
+
+        def weigh(ti):
+            grouped[ti] = vector_tile([P, P * PACK], BF16, "grouped")
+            nc.vector.tensor_tensor(
+                out=grouped[ti][:].rearrange("p (i t) -> p i t", t=PACK),
+                in0=turned[ti][:].rearrange("p t i -> p i t"),
+                in1=fj_cols[:].unsqueeze(1).to_broadcast([P, P, PACK]),
+                op=ALU.mult,
             )
 
         def quantise(ti):
@@ -212,16 +203,16 @@ def tile_list_unit_rows_listed_features_pl_kernel(
         )
         normalise(0)
         row_statistics(1)
-        for step in range(TILES + 4):
+        for step in range(TILES + 5):
             for stage, ti in (
-                (pick, step),
                 (row_statistics, step + 2),
+                (turn, step - 2),
+                (quantise, step - 3),
+                (second_product, step - 4),
                 (normalise, step + 1),
-                (turn, step - 1),
-                (quantise, step - 2),
-                (planes, step - 4),
-                (second_product, step - 3),
-                (round_once, step),
+                (pick, step),
+                (weigh, step - 2),
+                (planes, step - 5),
             ):
                 if 0 <= ti < TILES:
                     stage(ti)

from contextlib import ExitStack

import concourse.mybir as mybir
from concourse.masks import make_identity

K, T, I, C, J, N = 512, 1024, 512, 1024, 512, 512
FLOPS = 2 * K * I * C + 2 * J * N * I

F32 = mybir.dt.float32
BF16 = mybir.dt.bfloat16
I32 = mybir.dt.int32
U32 = mybir.dt.uint32
U16 = mybir.dt.uint16
U8 = mybir.dt.uint8
FP8X4 = mybir.dt.float8_e4m3fn_x4
FP4X4 = mybir.dt.float4_e2m1fn_x4
ACT = mybir.ActivationFunctionType
ALU = mybir.AluOpType

P = 128
PACK = 4
BANK = 512
TILES = I // P
EPS = 0.01
ON_VECTOR = ((0, 0), (0, 1), (1, 1), (2, 1))


def load_scale_rows(queue, plane, rows, quadrant):
    queue.dma_start(
        out=plane[32 * quadrant : 32 * quadrant + 4, :].bitcast(I32),
        in_=rows[4 * quadrant : 4 * quadrant + 4, :].bitcast(I32),
    )


def tile_list_unit_rows_listed_features_pl_kernel(
    tc, xt_words, xt_scales, wc_words, wc_scales, fj, wo_words, wo_scales, offs, offs2, out_0, out_1, out_2
):
    nc = tc.nc
    with ExitStack() as ctx:
        keep = ctx.enter_context(tc.tile_pool(name="keep", bufs=1))
        work = ctx.enter_context(tc.tile_pool(name="work", bufs=4))
        vector_ring = ctx.enter_context(tc.tile_pool(name="vector_ring", bufs=28))
        scalar_ring = ctx.enter_context(tc.tile_pool(name="scalar_ring", bufs=9))
        psum = ctx.enter_context(tc.psum_pool(name="psum", bufs=8))

        token_list = keep.tile([P, I // 16], U16)
        feature_list = keep.tile([P, J // 16], U16)
        x_words = keep.tile([P, T], I32, align_bytes=64)
        x_plane = keep.tile([P, T], U8, align_bytes=64)
        wc_codes = keep.tile([P, 2 * C], U8, align_bytes=64)
        wc_plane = keep.tile([P, C], U8, align_bytes=64)
        wo_raw = keep.tile([P, N], I32, align_bytes=64)
        wo_raw_plane = keep.tile([P, N], U8, align_bytes=64)
        fj_cols = keep.tile([P, PACK], F32)
        ident = keep.tile([P, P], F32)
        warm_in = keep.tile([P, 1], F32)
        warm_out = keep.tile([P, 1], F32)
        y_words = keep.tile([P, I], I32, align_bytes=64)
        y_plane = keep.tile([P, I], U8, align_bytes=64)

        nc.vector.memset(x_plane[:].bitcast(I32), 0)
        nc.vector.memset(wc_plane[:].bitcast(I32), 0)
        nc.vector.memset(warm_in[:], 1.0)
        nc.vector.memset(wo_raw_plane[:].bitcast(I32), 0)

        nc.sync.dma_start(token_list[:], offs2)
        for q in range(4):
            load_scale_rows(nc.scalar if q < 2 else nc.sync, x_plane, xt_scales[0], q)
        nc.sync.dma_start(out=x_words[:], in_=xt_words[0].rearrange("p n t -> p (n t)").bitcast(I32))
        nc.sync.dma_start(out=wc_codes[:].bitcast(I32), in_=wc_words[0].bitcast(I32))
        for q in range(4):
            load_scale_rows(nc.sync, wc_plane, wc_scales[0], q)
        nc.sync.dma_start(feature_list[:], offs)
        nc.sync.dma_start(out=wo_raw[:], in_=wo_words[0].rearrange("p n t -> p (n t)").bitcast(I32))
        for q in range(4):
            load_scale_rows(nc.sync, wo_raw_plane, wo_scales[0], q)
        nc.sync.dma_start(out=fj_cols[:], in_=fj.rearrange("(p t) o -> p (t o)", t=PACK))

        nc.scalar.activation(out=warm_out[:], in_=warm_in[:], func=ACT.Abs_reciprocal_sqrt)
        make_identity(nc, ident[:])

        def vector_tile(shape, dtype, name):
            return vector_ring.tile(shape, dtype, align_bytes=64, name=name, tag="vector")

        def scalar_tile(shape, dtype, name):
            return scalar_ring.tile(shape, dtype, align_bytes=64, name=name, tag="scalar")

        xg_plane = vector_tile([P, I], U8, "xg_plane")
        nc.vector.tensor_copy(out=xg_plane[:], in_=x_plane[:].indirect(token_list[:]))
        xg_words = []
        for ti in range(TILES):
            picks = token_list[:, 8 * ti : 8 * ti + 8]
            xg_words.append(vector_tile([P, P], I32, "xg_words"))
            nc.vector.tensor_copy(out=xg_words[ti][:].bitcast(U32), in_=x_words[:].bitcast(U32).indirect(picks))

        y_tiles, turned, grouped, z_first = {}, {}, {}, []
        z_banks, u_tiles, inv_rms, picked, uw_words, uw_plane = {}, {}, {}, {}, {}, {}

        def first_product(ti):
            z_banks[ti] = []
            for h in range(C // BANK):
                bank = psum.tile([P, BANK], F32, name="bank")
                nc.tensor.matmul_mx(
                    out=bank[:],
                    lhsT=xg_words[ti][:].bitcast(FP8X4),
                    lhsT_scale=xg_plane[:, P * ti : P * (ti + 1)],
                    rhs=wc_codes[:, 2 * BANK * h : 2 * BANK * (h + 1)].bitcast(FP4X4),
                    rhs_scale=wc_plane[:, BANK * h : BANK * (h + 1)],
                    start=True,
                    stop=True,
                )
                z_banks[ti].append(bank)

        def row_statistics(ti):
            stats = work.tile([P, 4], F32, name="stats")
            for h in range(C // BANK):
                squares = work.tile([P, BANK], BF16, name="squares")
                nc.scalar.activation(
                    out=squares[:], in_=z_banks[ti][h][:], func=ACT.Square, scale=C**-0.5, accum_out=stats[:, h : h + 1]
                )
                if h == 0:
                    nc.scalar.activation(out=stats[:, 2:3], in_=stats[:, 0:1], func=ACT.Copy, bias=EPS)
                if ti == 0:
                    z_first.append(vector_tile([P, BANK], F32, "z_first"))
                    nc.vector.tensor_copy(out=z_first[h][:], in_=z_banks[ti][h][:])
            nc.scalar.activation(out=stats[:, 3:4], in_=stats[:, 1:2], func=ACT.Abs_reciprocal_sqrt, bias=stats[:, 2:3])
            inv_rms[ti] = stats[:, 3:4]

        def normalise(ti):
            u_tiles[ti] = vector_tile([P, C], F32, "u") if (ti, 1) in ON_VECTOR else scalar_tile([P, C], F32, "u")
            for h in range(C // BANK):
                half = u_tiles[ti][:, BANK * h : BANK * (h + 1)]
                if (ti, h) in ON_VECTOR:
                    nc.vector.tensor_scalar(out=half, in0=z_first[h][:] if ti == 0 else z_banks[ti][h][:], scalar1=inv_rms[ti], scalar2=None, op0=ALU.mult)
                else:
                    nc.scalar.activation(out=half, in_=z_banks[ti][h][:], func=ACT.Copy, scale=inv_rms[ti])

        def pick(ti):
            picked[ti] = vector_tile([P, J], F32, "picked")
            nc.vector.tensor_copy(out=picked[ti][:], in_=u_tiles[ti][:].indirect(feature_list[:]))

        def turn(ti):
            turned[ti] = psum.tile([P, PACK, P], F32, name="bank")
            for t in range(PACK):
                nc.tensor.transpose(turned[ti][:, t, :], picked[ti][:, t:J:PACK], ident[:])

        def weigh(ti):
            grouped[ti] = vector_tile([P, P * PACK], BF16, "grouped")
            nc.vector.tensor_tensor(
                out=grouped[ti][:].rearrange("p (i t) -> p i t", t=PACK),
                in0=turned[ti][:].rearrange("p t i -> p i t"),
                in1=fj_cols[:].unsqueeze(1).to_broadcast([P, P, PACK]),
                op=ALU.mult,
            )

        def quantise(ti):
            uw_words[ti] = vector_tile([P, P], I32, "uw_words")
            uw_plane[ti] = work.tile([P, P], U8, align_bytes=64, name="uw_plane")
            nc.vector.quantize_mx(out=uw_words[ti][:].bitcast(FP8X4), scales=uw_plane[ti][:], in_=grouped[ti][:])

        def second_product(ti):
            cols = slice(P * ti, P * (ti + 1))
            bank = psum.tile([P, PACK, P], F32, name="bank")
            for t in range(PACK):
                nc.tensor.matmul_mx(
                    out=bank[:, t, :],
                    lhsT=wo_codes[:, P * t : P * (t + 1)].bitcast(FP8X4),
                    lhsT_scale=wo_plane[:, P * t : P * (t + 1)],
                    rhs=uw_words[ti][:].bitcast(FP8X4),
                    rhs_scale=uw_plane[ti][:],
                    start=True,
                    stop=True,
                )
            y = scalar_tile([P, PACK, P], F32, "y")
            nc.scalar.copy(out=y[:], in_=bank[:])
            nc.sync.dma_start(out=out_0.rearrange("(p t) i -> p t i", t=PACK)[:, :, cols], in_=y[:])
            y_tiles[ti] = y

        def planes(ti):
            cols = slice(P * ti, P * (ti + 1))
            y = y_tiles[ti]
            y_grouped = vector_tile([P, P * PACK], BF16, "y_grouped")
            nc.vector.tensor_copy(
                out=y_grouped[:].rearrange("p (c i t) -> p c t i", i=4, t=PACK),
                in_=y[:].rearrange("p t (c i) -> p c t i", i=4),
            )
            nc.vector.quantize_mx(out=y_words[:, cols].bitcast(FP8X4), scales=y_plane[:, cols], in_=y_grouped[:])
            if ti != 1:
                span = slice(P * (ti - (ti == 2)), P * (ti + 1))
                nc.sync.dma_start(out=out_1[0].rearrange("p i t -> p (i t)").bitcast(I32)[:, span], in_=y_words[:, span])

        for ti in range(TILES):
            first_product(ti)
        wo_codes = vector_tile([P, N], I32, "wo_codes")
        nc.vector.tensor_copy(
            out=wo_codes[:].rearrange("p (t c i) -> p c t i", t=PACK, i=4),
            in_=wo_raw[:].rearrange("p (c i t) -> p c t i", t=PACK, i=4),
        )
        row_statistics(0)
        wo_plane = vector_tile([P, N], U8, "wo_plane")
        nc.vector.tensor_copy(
            out=wo_plane[:].rearrange("p (t m) -> p t m", t=PACK), in_=wo_raw_plane[:].rearrange("p (m t) -> p t m", t=PACK)
        )
        normalise(0)
        row_statistics(1)
        for step in range(TILES + 5):
            for stage, ti in (
                (row_statistics, step + 2),
                (turn, step - 2),
                (quantise, step - 3),
                (second_product, step - 4),
                (normalise, step + 1),
                (pick, step),
                (weigh, step - 2),
                (planes, step - 5),
            ):
                if 0 <= ti < TILES:
                    stage(ti)

        for q in range(4):
            (nc.sync if q % 2 else nc.scalar).dma_start(
                out=out_2[0][4 * q : 4 * q + 4, :].bitcast(I32), in_=y_plane[32 * q : 32 * q + 4, :].bitcast(I32)
            )
